import numpy as np
import ml_dtypes

BF16 = ml_dtypes.bfloat16


def bf(x):
    return np.asarray(x, np.float32).astype(BF16)


def f32(x):
    return np.asarray(x, np.float32)


def f64(x):
    return np.asarray(x).astype(np.float64)


def striped(idx):
    return np.tile(idx.reshape(-1, 16).T, (8, 1))


def rows(idx, k):
    return np.tile(idx, (k, 1))


def look(tab, idx):
    return np.take_along_axis(f64(tab), rows(idx, len(tab)), axis=1)


K, S, V, N = 128, 256, 64, 64


def setup_inputs():
    return {"tab": f32(np.random.standard_normal((K, S))), "y": f32(np.random.standard_normal((K, V))), "offs": striped(np.random.permutation(S)[:N])}


def reference(tab, y, offs):
    idx = offs[:16].T.reshape(-1)
    t = look(tab, idx)
    x = np.maximum(t, 0.0) * f64(y)
    return x

@@ -1,0 +1,24 @@
+import concourse.mybir as mybir
+
+ROWS, TABLE_COLUMNS, PICKED = 128, 256, 64
+F32, U16 = mybir.dt.float32, mybir.dt.uint16
+
+FLOPS = 2 * ROWS * PICKED
+
+
+def tile_lookup_gate_relu_out_kernel(tc, tab, y, offs, out):
+    nc = tc.nc
+    with tc.tile_pool(name="held", bufs=1) as held:
+        offsets = held.tile([ROWS, PICKED // 16], U16)
+        table = held.tile([ROWS, TABLE_COLUMNS], F32)
+        stream = held.tile([ROWS, PICKED], F32)
+        gate = held.tile([ROWS, PICKED], F32)
+        product = held.tile([ROWS, PICKED], F32)
+
+        nc.sync.dma_start(offsets[:], offs)
+        nc.sync.dma_start(table[:], tab)
+        nc.sync.dma_start(stream[:], y)
+
+        nc.scalar.activation(gate[:], table[:].indirect(offsets[:]), mybir.ActivationFunctionType.Relu)
+        nc.vector.tensor_tensor(product[:], gate[:], stream[:], mybir.AluOpType.mult)
+        nc.sync.dma_start(out, product[:])

@@ -19,6 +19,11 @@ def tile_lookup_gate_relu_out_kernel(tc, tab, y, offs, out):
         nc.sync.dma_start(table[:], tab)
         nc.sync.dma_start(stream[:], y)
 
+        zero = held.tile([ROWS, 1], F32)
+        warmed = held.tile([ROWS, 1], F32)
+        nc.vector.memset(zero[:], 0.0)
+        nc.scalar.activation(warmed[:], zero[:], mybir.ActivationFunctionType.Relu)
+
         nc.scalar.activation(gate[:], table[:].indirect(offsets[:]), mybir.ActivationFunctionType.Relu)
         nc.vector.tensor_tensor(product[:], gate[:], stream[:], mybir.AluOpType.mult)
         nc.sync.dma_start(out, product[:])

@@ -15,8 +15,8 @@ def tile_lookup_gate_relu_out_kernel(tc, tab, y, offs, out):
         gate = held.tile([ROWS, PICKED], F32)
         product = held.tile([ROWS, PICKED], F32)
 
-        nc.sync.dma_start(offsets[:], offs)
         nc.sync.dma_start(table[:], tab)
+        nc.sync.dma_start(offsets[:], offs)
         nc.sync.dma_start(stream[:], y)
 
         zero = held.tile([ROWS, 1], F32)

import concourse.mybir as mybir

ROWS, TABLE_COLUMNS, PICKED = 128, 256, 64
F32, U16 = mybir.dt.float32, mybir.dt.uint16

FLOPS = 2 * ROWS * PICKED


def tile_lookup_gate_relu_out_kernel(tc, tab, y, offs, out):
    nc = tc.nc
    with tc.tile_pool(name="held", bufs=1) as held:
        offsets = held.tile([ROWS, PICKED // 16], U16)
        table = held.tile([ROWS, TABLE_COLUMNS], F32)
        stream = held.tile([ROWS, PICKED], F32)
        gate = held.tile([ROWS, PICKED], F32)
        product = held.tile([ROWS, PICKED], F32)

        nc.sync.dma_start(table[:], tab)
        nc.sync.dma_start(offsets[:], offs)
        nc.sync.dma_start(stream[:], y)

        zero = held.tile([ROWS, 1], F32)
        warmed = held.tile([ROWS, 1], F32)
        nc.vector.memset(zero[:], 0.0)
        nc.scalar.activation(warmed[:], zero[:], mybir.ActivationFunctionType.Relu)

        nc.scalar.activation(gate[:], table[:].indirect(offsets[:]), mybir.ActivationFunctionType.Relu)
        nc.vector.tensor_tensor(product[:], gate[:], stream[:], mybir.AluOpType.mult)
        nc.sync.dma_start(out, product[:])
